import numpy as np, ml_dtypes
CORES = [242,247,114,119]
N = 4
NH, QP = 2, 128
def setup_inputs(rng):
    return {"q": rng.standard_normal((N, 128, NH * QP), dtype=np.float32).astype(ml_dtypes.bfloat16), "k": rng.standard_normal((N, 128, NH * 128), dtype=np.float32).astype(ml_dtypes.bfloat16), "v": rng.standard_normal((N, 128, NH * 128), dtype=np.float32).astype(ml_dtypes.bfloat16)}
def setup_inputs_big(rng):
    d = setup_inputs(rng)
    for k in ("q", "k", "v"): d[k] = (d[k].astype(np.float32) * 1024.0).astype(d[k].dtype)
    return d
def setup_inputs_small(rng):
    d = setup_inputs(rng)
    for k in ("q", "k", "v"): d[k] = (d[k].astype(np.float32) * (1 / 1024.0)).astype(d[k].dtype)
    return d
def setup_inputs_apart(rng):
    d = setup_inputs(rng)
    f = (10.0 ** rng.permutation(np.linspace(-1.5, 1.5, N))).astype(np.float32).reshape(N, 1, 1)
    for k in ("q", "k", "v"): d[k] = (d[k].astype(np.float32) * f).astype(d[k].dtype)
    return d
def reference(q, k, v):
    Q, K, V = q.astype(np.float64), k.astype(np.float64), v.astype(np.float64)
    y = np.zeros((N, 128, NH * QP))
    for r in range(N):
        for h in range(NH):
            for j in range(N):
                S = np.maximum(K[j][:, 128 * h:128 * h + 128].T @ Q[r][:, QP * h:QP * h + QP], 0.0)
                y[r][:, QP * h:QP * h + QP] += V[j][:, 128 * h:128 * h + 128].T @ S
    return {"y": y.astype(ml_dtypes.bfloat16 if q.dtype != np.float64 else np.float64)}

@@ -1,0 +1,112 @@
+from concourse.mybir import AluOpType
+
+N, NH, W = 4, 2, 128
+KVW = 2 * NH * W
+NSB = 4
+
+SCRATCH = {
+    "kv": ("sbuf", [128, N * KVW], "bfloat16"),
+    "qs": ("sbuf", [128, NH * W], "bfloat16"),
+    "zero": ("sbuf", [128, W], "float32"),
+    "ss": ("sbuf", [128, N * NH * W], "bfloat16"),
+    "ysb": ("sbuf", [128, NH * W], "bfloat16"),
+    "op0": ("psum", [128, 512], "float32"),
+    "op1": ("psum", [128, 512], "float32"),
+}
+for _b in range(NSB):
+    SCRATCH["sp%d" % _b] = ("psum", [128, 512], "float32")
+
+SEMAPHORES = (["ldkv", "ldq", "sent", "zf", "cp", "st", "o0", "o1"]
+              + ["arr%d" % j for j in range(N)]
+              + ["s%d" % t for t in range(N * NH)]
+              + ["r%d" % t for t in range(N * NH)])
+
+
+def _engines(mask):
+    return [e for e in range(mask.bit_length()) if (mask >> e) & 1]
+
+
+def _mask_of(engines):
+    n = 1
+    while 2 * n <= len(engines):
+        n *= 2
+    m = 0
+    for e in engines[:n]:
+        m |= 1 << e
+    return m, n
+
+
+def rank_program(g, core, T, topo):
+    rank = T.rank_of(core)
+    if rank is None:
+        return
+
+    def one_chip(a, b):
+        return topo.host(a) == topo.host(b) and topo.chip(a) == topo.chip(b)
+
+    def mask_for(src, dst):
+        can = _engines(topo.mask(src, dst))
+        if not one_chip(src, dst):
+            return _mask_of(can)
+        leaving = 0
+        for c in T.cores:
+            if not one_chip(src, c):
+                leaving |= topo.mask(src, c)
+        spare = [e for e in can if not (leaving >> e) & 1]
+        return _mask_of(spare if spare else can)
+
+    others = [c for c in T.cores if c != core]
+    near = [c for c in others if one_chip(c, core)]
+    far = [c for c in others if not one_chip(c, core)]
+    order = ([c for c in far if topo.die(c) == topo.die(core)] + near
+             + [c for c in far if topo.die(c) != topo.die(core)])
+
+    own = rank * KVW
+    g.sync.dma_start(T.kv[:, own:own + NH * W], T.k[:]).then_inc(T.sem.ldkv, 16)
+    g.scalar.dma_start(T.kv[:, own + NH * W:own + KVW], T.v[:]).then_inc(T.sem.ldkv, 16)
+    g.sync.dma_start(T.qs[:], T.q[:]).then_inc(T.sem.ldq, 16)
+
+    g.wait_ge(T.sem.ldkv, 32)
+    left = 0
+    for c in order:
+        rid, pid = topo.addr(c, core)
+        m, n = mask_for(core, c)
+        g.remote_dma(out_ap=T.kv[:, own:own + KVW], in_ap=T.kv[:, own:own + KVW], remote_sem=T.sem["arr%d" % rank],
+                     local_sem=T.sem.sent, pid=pid, routing_id=rid, dma_engine_mask=m)
+        left += n
+
+    v, t = g.vector, g.tensor
+    v.memset(T.zero[:], 0.0).then_inc(T.sem.zf, 1)
+    v.wait_ge(T.sem.zf, 1)
+    t.wait_ge(T.sem.ldkv, 32)
+    t.wait_ge(T.sem.ldq, 16)
+    blocks = [core] + order
+    for i, c in enumerate(blocks):
+        j = T.rank_of(c)
+        kcol, vcol = j * KVW, j * KVW + NH * W
+        last = i == len(blocks) - 1
+        if c != core:
+            t.wait_ge(T.sem["arr%d" % j], mask_for(c, core)[1])
+        for h in range(NH):
+            tile = NH * i + h
+            sp = T["sp%d" % (tile % NSB)]
+            t.matmul(sp[:, 0:W], T.kv[:, kcol + h * W:kcol + (h + 1) * W], T.qs[:, h * W:(h + 1) * W],
+                     True, True).then_inc(T.sem["s%d" % tile], 1)
+            v.wait_ge(T.sem["s%d" % tile], 1)
+            v.tensor_tensor(T.ss[:, tile * W:(tile + 1) * W], sp[:, 0:W], T.zero[:],
+                            AluOpType.max).then_inc(T.sem["r%d" % tile], 1)
+        for h in range(NH):
+            tile = NH * i + h
+            t.wait_ge(T.sem["r%d" % tile], 1)
+            mm = t.matmul(T["op%d" % h][:, 0:W], T.kv[:, vcol + h * W:vcol + (h + 1) * W],
+                          T.ss[:, tile * W:(tile + 1) * W], i == 0, last)
+            if last:
+                mm.then_inc(T.sem["o%d" % h], 1)
+    for h in range(NH):
+        v.wait_ge(T.sem["o%d" % h], 1)
+        v.tensor_copy(T.ysb[:, h * W:(h + 1) * W], T["op%d" % h][:, 0:W]).then_inc(T.sem.cp, 1)
+
+    g.sync.wait_ge(T.sem.cp, NH)
+    g.sync.dma_start(T.y[:], T.ysb[:]).then_inc(T.sem.st, 16)
+    g.sync.wait_ge(T.sem.st, 16)
+    g.wait_ge(T.sem.sent, left)

@@ -16,7 +16,8 @@ SCRATCH = {
 for _b in range(NSB):
     SCRATCH["sp%d" % _b] = ("psum", [128, 512], "float32")
 
-SEMAPHORES = (["ldkv", "ldq", "sent", "zf", "cp", "st", "o0", "o1"]
+SEMAPHORES = (["ldk", "ldv", "ldq", "sent", "zf", "cp", "st", "o0", "o1"]
+              + ["ark%d" % j for j in range(N)]
               + ["arr%d" % j for j in range(N)]
               + ["s%d" % t for t in range(N * NH)]
               + ["r%d" % t for t in range(N * NH)])
@@ -58,50 +59,73 @@ def rank_program(g, core, T, topo):
     others = [c for c in T.cores if c != core]
     near = [c for c in others if one_chip(c, core)]
     far = [c for c in others if not one_chip(c, core)]
-    order = ([c for c in far if topo.die(c) == topo.die(core)] + near
-             + [c for c in far if topo.die(c) != topo.die(core)])
+    far_same = [c for c in far if topo.die(c) == topo.die(core)]
+    far_cross = [c for c in far if topo.die(c) != topo.die(core)]
 
     own = rank * KVW
-    g.sync.dma_start(T.kv[:, own:own + NH * W], T.k[:]).then_inc(T.sem.ldkv, 16)
-    g.scalar.dma_start(T.kv[:, own + NH * W:own + KVW], T.v[:]).then_inc(T.sem.ldkv, 16)
+    kpart, vpart, both = T.kv[:, own:own + NH * W], T.kv[:, own + NH * W:own + KVW], T.kv[:, own:own + KVW]
+    g.sync.dma_start(kpart, T.k[:]).then_inc(T.sem.ldk, 16)
+    g.scalar.dma_start(vpart, T.v[:]).then_inc(T.sem.ldv, 16)
     g.sync.dma_start(T.qs[:], T.q[:]).then_inc(T.sem.ldq, 16)
 
-    g.wait_ge(T.sem.ldkv, 32)
-    left = 0
-    for c in order:
+    left = [0]
+
+    def send(c, ap, sem):
         rid, pid = topo.addr(c, core)
         m, n = mask_for(core, c)
-        g.remote_dma(out_ap=T.kv[:, own:own + KVW], in_ap=T.kv[:, own:own + KVW], remote_sem=T.sem["arr%d" % rank],
-                     local_sem=T.sem.sent, pid=pid, routing_id=rid, dma_engine_mask=m)
-        left += n
+        g.remote_dma(out_ap=ap, in_ap=ap, remote_sem=T.sem[sem % rank], local_sem=T.sem.sent,
+                     pid=pid, routing_id=rid, dma_engine_mask=m)
+        left[0] += n
+
+    g.wait_ge(T.sem.ldk, 16)
+    for c in far_cross:
+        send(c, kpart, "ark%d")
+    g.wait_ge(T.sem.ldv, 16)
+    for c in far_same + near:
+        send(c, both, "arr%d")
+    for c in far_cross:
+        send(c, vpart, "arr%d")
 
     v, t = g.vector, g.tensor
     v.memset(T.zero[:], 0.0).then_inc(T.sem.zf, 1)
     v.wait_ge(T.sem.zf, 1)
-    t.wait_ge(T.sem.ldkv, 32)
-    t.wait_ge(T.sem.ldq, 16)
-    blocks = [core] + order
-    for i, c in enumerate(blocks):
+    steps = ([("S", core), ("O", core)] + [("S", c) for c in far_cross + far_same + near]
+             + [("O", c) for c in far_same + near + far_cross])
+    n_o = len([s for s in steps if s[0] == "O"])
+    tile_of, seen_o = {}, 0
+    for what, c in steps:
         j = T.rank_of(c)
         kcol, vcol = j * KVW, j * KVW + NH * W
-        last = i == len(blocks) - 1
-        if c != core:
-            t.wait_ge(T.sem["arr%d" % j], mask_for(c, core)[1])
-        for h in range(NH):
-            tile = NH * i + h
-            sp = T["sp%d" % (tile % NSB)]
-            t.matmul(sp[:, 0:W], T.kv[:, kcol + h * W:kcol + (h + 1) * W], T.qs[:, h * W:(h + 1) * W],
-                     True, True).then_inc(T.sem["s%d" % tile], 1)
-            v.wait_ge(T.sem["s%d" % tile], 1)
-            v.tensor_tensor(T.ss[:, tile * W:(tile + 1) * W], sp[:, 0:W], T.zero[:],
-                            AluOpType.max).then_inc(T.sem["r%d" % tile], 1)
-        for h in range(NH):
-            tile = NH * i + h
-            t.wait_ge(T.sem["r%d" % tile], 1)
-            mm = t.matmul(T["op%d" % h][:, 0:W], T.kv[:, vcol + h * W:vcol + (h + 1) * W],
-                          T.ss[:, tile * W:(tile + 1) * W], i == 0, last)
-            if last:
-                mm.then_inc(T.sem["o%d" % h], 1)
+        if what == "S":
+            if c == core:
+                t.wait_ge(T.sem.ldk, 16)
+                t.wait_ge(T.sem.ldq, 16)
+            else:
+                t.wait_ge(T.sem[("ark%d" if c in far_cross else "arr%d") % j], mask_for(c, core)[1])
+            tile_of[c] = NH * len(tile_of)
+            for h in range(NH):
+                tile = tile_of[c] + h
+                sp = T["sp%d" % (tile % NSB)]
+                if tile >= NSB:
+                    t.wait_ge(T.sem["r%d" % (tile - NSB)], 1)
+                t.matmul(sp[:, 0:W], T.kv[:, kcol + h * W:kcol + (h + 1) * W], T.qs[:, h * W:(h + 1) * W],
+                         True, True).then_inc(T.sem["s%d" % tile], 1)
+                v.wait_ge(T.sem["s%d" % tile], 1)
+                v.tensor_tensor(T.ss[:, tile * W:(tile + 1) * W], sp[:, 0:W], T.zero[:],
+                                AluOpType.max).then_inc(T.sem["r%d" % tile], 1)
+        else:
+            if c == core:
+                t.wait_ge(T.sem.ldv, 16)
+            elif c in far_cross:
+                t.wait_ge(T.sem["arr%d" % j], mask_for(c, core)[1])
+            seen_o += 1
+            for h in range(NH):
+                tile = tile_of[c] + h
+                t.wait_ge(T.sem["r%d" % tile], 1)
+                mm = t.matmul(T["op%d" % h][:, 0:W], T.kv[:, vcol + h * W:vcol + (h + 1) * W],
+                              T.ss[:, tile * W:(tile + 1) * W], seen_o == 1, seen_o == n_o)
+                if seen_o == n_o:
+                    mm.then_inc(T.sem["o%d" % h], 1)
     for h in range(NH):
         v.wait_ge(T.sem["o%d" % h], 1)
         v.tensor_copy(T.ysb[:, h * W:(h + 1) * W], T["op%d" % h][:, 0:W]).then_inc(T.sem.cp, 1)
@@ -109,4 +133,4 @@ def rank_program(g, core, T, topo):
     g.sync.wait_ge(T.sem.cp, NH)
     g.sync.dma_start(T.y[:], T.ysb[:]).then_inc(T.sem.st, 16)
     g.sync.wait_ge(T.sem.st, 16)
-    g.wait_ge(T.sem.sent, left)
+    g.wait_ge(T.sem.sent, left[0])

@@ -1,3 +1,4 @@
+from concourse.bass import DstId, RemoteDMATransfer
 from concourse.mybir import AluOpType
 
 N, NH, W = 4, 2, 128
@@ -16,9 +17,11 @@ SCRATCH = {
 for _b in range(NSB):
     SCRATCH["sp%d" % _b] = ("psum", [128, 512], "float32")
 
-SEMAPHORES = (["ldk", "ldv", "ldq", "sent", "zf", "cp", "st", "o0", "o1"]
-              + ["ark%d" % j for j in range(N)]
-              + ["arr%d" % j for j in range(N)]
+SEMAPHORES = (["ldk", "ldq", "sent", "zf"]
+              + ["%s%d" % (n, h) for n in ("ldv", "cp", "st", "o") for h in range(NH)]
+              + ["k%d" % j for j in range(N)]
+              + ["v%d" % j for j in range(N)]
+              + ["v%d_%d" % (j, h) for j in range(N) for h in range(NH)]
               + ["s%d" % t for t in range(N * NH)]
               + ["r%d" % t for t in range(N * NH)])
 
@@ -62,75 +65,110 @@ def rank_program(g, core, T, topo):
     far_same = [c for c in far if topo.die(c) == topo.die(core)]
     far_cross = [c for c in far if topo.die(c) != topo.die(core)]
 
-    own = rank * KVW
-    kpart, vpart, both = T.kv[:, own:own + NH * W], T.kv[:, own + NH * W:own + KVW], T.kv[:, own:own + KVW]
-    g.sync.dma_start(kpart, T.k[:]).then_inc(T.sem.ldk, 16)
-    g.scalar.dma_start(vpart, T.v[:]).then_inc(T.sem.ldv, 16)
-    g.sync.dma_start(T.qs[:], T.q[:]).then_inc(T.sem.ldq, 16)
+    def kcols(j, h0=0, h1=NH):
+        return T.kv[:, j * KVW + h0 * W:j * KVW + h1 * W]
+
+    def vcols(j, h0=0, h1=NH):
+        return T.kv[:, j * KVW + (NH + h0) * W:j * KVW + (NH + h1) * W]
+
+    queues = [g.sync, g.scalar]
+    g.sync.dma_start(vcols(rank, 0, 1), T.v[:, 0:W]).then_inc(T.sem.ldv0, 16)
+    g.scalar.dma_start(kcols(rank), T.k[:]).then_inc(T.sem.ldk, 16)
+    g.sync.dma_start(vcols(rank, 1, NH), T.v[:, W:NH * W]).then_inc(T.sem.ldv1, 16)
+    g.scalar.dma_start(T.qs[:], T.q[:]).then_inc(T.sem.ldq, 16)
 
     left = [0]
 
-    def send(c, ap, sem):
-        rid, pid = topo.addr(c, core)
-        m, n = mask_for(core, c)
-        g.remote_dma(out_ap=ap, in_ap=ap, remote_sem=T.sem[sem % rank], local_sem=T.sem.sent,
-                     pid=pid, routing_id=rid, dma_engine_mask=m)
-        left[0] += n
+    def send(items):
+        used, disjoint = 0, True
+        for c, ap, sem in items:
+            m = mask_for(core, c)[0]
+            disjoint = disjoint and not (used & m)
+            used |= m
+        if len(items) > 1 and disjoint:
+            trs = []
+            for c, ap, sem in items:
+                rid, pid = topo.addr(c, core)
+                m, n = mask_for(core, c)
+                trs.append(RemoteDMATransfer(dst_ids=[DstId(rid=rid, pnc=pid)], dma_engine_mask=m,
+                                             remote_sem=T.sem[sem], src=ap, dst=ap))
+                left[0] += n
+            g.remote_dma_fused(trs, local_sem=T.sem.sent)
+            return
+        for c, ap, sem in items:
+            rid, pid = topo.addr(c, core)
+            m, n = mask_for(core, c)
+            g.remote_dma(out_ap=ap, in_ap=ap, remote_sem=T.sem[sem], local_sem=T.sem.sent,
+                         pid=pid, routing_id=rid, dma_engine_mask=m)
+            left[0] += n
 
+    g.wait_ge(T.sem.ldv0, 16)
+    send([(c, vcols(rank, 0, 1), "v%d_0" % rank) for c in far_same])
     g.wait_ge(T.sem.ldk, 16)
-    for c in far_cross:
-        send(c, kpart, "ark%d")
-    g.wait_ge(T.sem.ldv, 16)
-    for c in far_same + near:
-        send(c, both, "arr%d")
-    for c in far_cross:
-        send(c, vpart, "arr%d")
+    send([(c, kcols(rank), "k%d" % rank) for c in far_same + near])
+    g.wait_ge(T.sem.ldv1, 16)
+    send([(c, vcols(rank), "v%d" % rank) for c in near])
+    send([(c, kcols(rank), "k%d" % rank) for c in far_cross])
+    send([(c, vcols(rank, 1, NH), "v%d_1" % rank) for c in far_same])
+    send([(c, vcols(rank, 1, NH), "v%d_1" % rank) for c in far_cross])
+    for c in far_same:
+        j = T.rank_of(c)
+        g.wait_ge(T.sem["v%d_0" % j], mask_for(c, core)[1])
+        send([(d, vcols(j, 0, 1), "v%d_0" % j) for d in near])
 
     v, t = g.vector, g.tensor
     v.memset(T.zero[:], 0.0).then_inc(T.sem.zf, 1)
     v.wait_ge(T.sem.zf, 1)
-    steps = ([("S", core), ("O", core)] + [("S", c) for c in far_cross + far_same + near]
-             + [("O", c) for c in far_same + near + far_cross])
-    n_o = len([s for s in steps if s[0] == "O"])
-    tile_of, seen_o = {}, 0
-    for what, c in steps:
+    heads = list(range(NH))
+    steps = ([("S", core, heads), ("O", core, heads)]
+             + [("S", c, heads) for c in near + far_same]
+             + [("O", c, [0]) for c in far_same] + [("O", c, heads) for c in near]
+             + [("S", c, heads) for c in far_cross]
+             + [("O", c, heads[1:]) for c in far_same] + [("O", c, heads) for c in far_cross])
+    n_o = [len([1 for s in steps if s[0] == "O" and h in s[2]]) for h in heads]
+    seen_o = [0 for h in heads]
+    tile_of = {}
+    for what, c, hs in steps:
         j = T.rank_of(c)
-        kcol, vcol = j * KVW, j * KVW + NH * W
         if what == "S":
             if c == core:
                 t.wait_ge(T.sem.ldk, 16)
                 t.wait_ge(T.sem.ldq, 16)
             else:
-                t.wait_ge(T.sem[("ark%d" if c in far_cross else "arr%d") % j], mask_for(c, core)[1])
+                t.wait_ge(T.sem["k%d" % j], mask_for(c, core)[1])
             tile_of[c] = NH * len(tile_of)
-            for h in range(NH):
+            for h in hs:
                 tile = tile_of[c] + h
                 sp = T["sp%d" % (tile % NSB)]
                 if tile >= NSB:
                     t.wait_ge(T.sem["r%d" % (tile - NSB)], 1)
-                t.matmul(sp[:, 0:W], T.kv[:, kcol + h * W:kcol + (h + 1) * W], T.qs[:, h * W:(h + 1) * W],
+                t.matmul(sp[:, 0:W], kcols(j, h, h + 1), T.qs[:, h * W:(h + 1) * W],
                          True, True).then_inc(T.sem["s%d" % tile], 1)
                 v.wait_ge(T.sem["s%d" % tile], 1)
                 v.tensor_tensor(T.ss[:, tile * W:(tile + 1) * W], sp[:, 0:W], T.zero[:],
                                 AluOpType.max).then_inc(T.sem["r%d" % tile], 1)
         else:
-            if c == core:
-                t.wait_ge(T.sem.ldv, 16)
-            elif c in far_cross:
-                t.wait_ge(T.sem["arr%d" % j], mask_for(c, core)[1])
-            seen_o += 1
-            for h in range(NH):
+            if c in near:
+                t.wait_ge(T.sem["v%d" % j], mask_for(c, core)[1])
+            for h in hs:
                 tile = tile_of[c] + h
+                if c == core:
+                    t.wait_ge(T.sem["ldv%d" % h], 16)
+                elif c in far:
+                    src = near[0] if (c in far_cross and h == 0) else c
+                    t.wait_ge(T.sem["v%d_%d" % (j, h)], mask_for(src, core)[1])
                 t.wait_ge(T.sem["r%d" % tile], 1)
-                mm = t.matmul(T["op%d" % h][:, 0:W], T.kv[:, vcol + h * W:vcol + (h + 1) * W],
-                              T.ss[:, tile * W:(tile + 1) * W], seen_o == 1, seen_o == n_o)
-                if seen_o == n_o:
+                seen_o[h] += 1
+                mm = t.matmul(T["op%d" % h][:, 0:W], vcols(j, h, h + 1),
+                              T.ss[:, tile * W:(tile + 1) * W], seen_o[h] == 1, seen_o[h] == n_o[h])
+                if seen_o[h] == n_o[h]:
                     mm.then_inc(T.sem["o%d" % h], 1)
-    for h in range(NH):
-        v.wait_ge(T.sem["o%d" % h], 1)
-        v.tensor_copy(T.ysb[:, h * W:(h + 1) * W], T["op%d" % h][:, 0:W]).then_inc(T.sem.cp, 1)
 
-    g.sync.wait_ge(T.sem.cp, NH)
-    g.sync.dma_start(T.y[:], T.ysb[:]).then_inc(T.sem.st, 16)
-    g.sync.wait_ge(T.sem.st, 16)
+    for h in heads:
+        v.wait_ge(T.sem["o%d" % h], 1)
+        v.tensor_copy(T.ysb[:, h * W:(h + 1) * W], T["op%d" % h][:, 0:W]).then_inc(T.sem["cp%d" % h], 1)
+        qu = queues[(NH - 1 - h) % 2]
+        qu.wait_ge(T.sem["cp%d" % h], 1)
+        qu.dma_start(T.y[:, h * W:(h + 1) * W], T.ysb[:, h * W:(h + 1) * W]).then_inc(T.sem["st%d" % h], 16)
+        qu.wait_ge(T.sem["st%d" % h], 16)
     g.wait_ge(T.sem.sent, left[0])

from concourse.bass import DstId, RemoteDMATransfer
from concourse.mybir import AluOpType

N, NH, W = 4, 2, 128
KVW = 2 * NH * W
NSB = 4

SCRATCH = {
    "kv": ("sbuf", [128, N * KVW], "bfloat16"),
    "qs": ("sbuf", [128, NH * W], "bfloat16"),
    "zero": ("sbuf", [128, W], "float32"),
    "ss": ("sbuf", [128, N * NH * W], "bfloat16"),
    "ysb": ("sbuf", [128, NH * W], "bfloat16"),
    "op0": ("psum", [128, 512], "float32"),
    "op1": ("psum", [128, 512], "float32"),
}
for _b in range(NSB):
    SCRATCH["sp%d" % _b] = ("psum", [128, 512], "float32")

SEMAPHORES = (["ldk", "ldq", "sent", "zf"]
              + ["%s%d" % (n, h) for n in ("ldv", "cp", "st", "o") for h in range(NH)]
              + ["k%d" % j for j in range(N)]
              + ["v%d" % j for j in range(N)]
              + ["v%d_%d" % (j, h) for j in range(N) for h in range(NH)]
              + ["s%d" % t for t in range(N * NH)]
              + ["r%d" % t for t in range(N * NH)])


def _engines(mask):
    return [e for e in range(mask.bit_length()) if (mask >> e) & 1]


def _mask_of(engines):
    n = 1
    while 2 * n <= len(engines):
        n *= 2
    m = 0
    for e in engines[:n]:
        m |= 1 << e
    return m, n


def rank_program(g, core, T, topo):
    rank = T.rank_of(core)
    if rank is None:
        return

    def one_chip(a, b):
        return topo.host(a) == topo.host(b) and topo.chip(a) == topo.chip(b)

    def mask_for(src, dst):
        can = _engines(topo.mask(src, dst))
        if not one_chip(src, dst):
            return _mask_of(can)
        leaving = 0
        for c in T.cores:
            if not one_chip(src, c):
                leaving |= topo.mask(src, c)
        spare = [e for e in can if not (leaving >> e) & 1]
        return _mask_of(spare if spare else can)

    others = [c for c in T.cores if c != core]
    near = [c for c in others if one_chip(c, core)]
    far = [c for c in others if not one_chip(c, core)]
    far_same = [c for c in far if topo.die(c) == topo.die(core)]
    far_cross = [c for c in far if topo.die(c) != topo.die(core)]

    def kcols(j, h0=0, h1=NH):
        return T.kv[:, j * KVW + h0 * W:j * KVW + h1 * W]

    def vcols(j, h0=0, h1=NH):
        return T.kv[:, j * KVW + (NH + h0) * W:j * KVW + (NH + h1) * W]

    queues = [g.sync, g.scalar]
    g.sync.dma_start(vcols(rank, 0, 1), T.v[:, 0:W]).then_inc(T.sem.ldv0, 16)
    g.scalar.dma_start(kcols(rank), T.k[:]).then_inc(T.sem.ldk, 16)
    g.sync.dma_start(vcols(rank, 1, NH), T.v[:, W:NH * W]).then_inc(T.sem.ldv1, 16)
    g.scalar.dma_start(T.qs[:], T.q[:]).then_inc(T.sem.ldq, 16)

    left = [0]

    def send(items):
        used, disjoint = 0, True
        for c, ap, sem in items:
            m = mask_for(core, c)[0]
            disjoint = disjoint and not (used & m)
            used |= m
        if len(items) > 1 and disjoint:
            trs = []
            for c, ap, sem in items:
                rid, pid = topo.addr(c, core)
                m, n = mask_for(core, c)
                trs.append(RemoteDMATransfer(dst_ids=[DstId(rid=rid, pnc=pid)], dma_engine_mask=m,
                                             remote_sem=T.sem[sem], src=ap, dst=ap))
                left[0] += n
            g.remote_dma_fused(trs, local_sem=T.sem.sent)
            return
        for c, ap, sem in items:
            rid, pid = topo.addr(c, core)
            m, n = mask_for(core, c)
            g.remote_dma(out_ap=ap, in_ap=ap, remote_sem=T.sem[sem], local_sem=T.sem.sent,
                         pid=pid, routing_id=rid, dma_engine_mask=m)
            left[0] += n

    g.wait_ge(T.sem.ldv0, 16)
    send([(c, vcols(rank, 0, 1), "v%d_0" % rank) for c in far_same])
    g.wait_ge(T.sem.ldk, 16)
    send([(c, kcols(rank), "k%d" % rank) for c in far_same + near])
    g.wait_ge(T.sem.ldv1, 16)
    send([(c, vcols(rank), "v%d" % rank) for c in near])
    send([(c, kcols(rank), "k%d" % rank) for c in far_cross])
    send([(c, vcols(rank, 1, NH), "v%d_1" % rank) for c in far_same])
    send([(c, vcols(rank, 1, NH), "v%d_1" % rank) for c in far_cross])
    for c in far_same:
        j = T.rank_of(c)
        g.wait_ge(T.sem["v%d_0" % j], mask_for(c, core)[1])
        send([(d, vcols(j, 0, 1), "v%d_0" % j) for d in near])

    v, t = g.vector, g.tensor
    v.memset(T.zero[:], 0.0).then_inc(T.sem.zf, 1)
    v.wait_ge(T.sem.zf, 1)
    heads = list(range(NH))
    steps = ([("S", core, heads), ("O", core, heads)]
             + [("S", c, heads) for c in near + far_same]
             + [("O", c, [0]) for c in far_same] + [("O", c, heads) for c in near]
             + [("S", c, heads) for c in far_cross]
             + [("O", c, heads[1:]) for c in far_same] + [("O", c, heads) for c in far_cross])
    n_o = [len([1 for s in steps if s[0] == "O" and h in s[2]]) for h in heads]
    seen_o = [0 for h in heads]
    tile_of = {}
    for what, c, hs in steps:
        j = T.rank_of(c)
        if what == "S":
            if c == core:
                t.wait_ge(T.sem.ldk, 16)
                t.wait_ge(T.sem.ldq, 16)
            else:
                t.wait_ge(T.sem["k%d" % j], mask_for(c, core)[1])
            tile_of[c] = NH * len(tile_of)
            for h in hs:
                tile = tile_of[c] + h
                sp = T["sp%d" % (tile % NSB)]
                if tile >= NSB:
                    t.wait_ge(T.sem["r%d" % (tile - NSB)], 1)
                t.matmul(sp[:, 0:W], kcols(j, h, h + 1), T.qs[:, h * W:(h + 1) * W],
                         True, True).then_inc(T.sem["s%d" % tile], 1)
                v.wait_ge(T.sem["s%d" % tile], 1)
                v.tensor_tensor(T.ss[:, tile * W:(tile + 1) * W], sp[:, 0:W], T.zero[:],
                                AluOpType.max).then_inc(T.sem["r%d" % tile], 1)
        else:
            if c in near:
                t.wait_ge(T.sem["v%d" % j], mask_for(c, core)[1])
            for h in hs:
                tile = tile_of[c] + h
                if c == core:
                    t.wait_ge(T.sem["ldv%d" % h], 16)
                elif c in far:
                    src = near[0] if (c in far_cross and h == 0) else c
                    t.wait_ge(T.sem["v%d_%d" % (j, h)], mask_for(src, core)[1])
                t.wait_ge(T.sem["r%d" % tile], 1)
                seen_o[h] += 1
                mm = t.matmul(T["op%d" % h][:, 0:W], vcols(j, h, h + 1),
                              T.ss[:, tile * W:(tile + 1) * W], seen_o[h] == 1, seen_o[h] == n_o[h])
                if seen_o[h] == n_o[h]:
                    mm.then_inc(T.sem["o%d" % h], 1)

    for h in heads:
        v.wait_ge(T.sem["o%d" % h], 1)
        v.tensor_copy(T.ysb[:, h * W:(h + 1) * W], T["op%d" % h][:, 0:W]).then_inc(T.sem["cp%d" % h], 1)
        qu = queues[(NH - 1 - h) % 2]
        qu.wait_ge(T.sem["cp%d" % h], 1)
        qu.dma_start(T.y[:, h * W:(h + 1) * W], T.ysb[:, h * W:(h + 1) * W]).then_inc(T.sem["st%d" % h], 16)
        qu.wait_ge(T.sem["st%d" % h], 16)
    g.wait_ge(T.sem.sent, left[0])
